import numpy as np
import ml_dtypes


def mxq(x, axis, fmt="e4m3"):
    dtype, down = {"e4m3": (ml_dtypes.float8_e4m3fn, 7), "e5m2": (ml_dtypes.float8_e5m2, 14)}[fmt]
    v = np.moveaxis(np.asarray(x, np.float32).astype(ml_dtypes.bfloat16).astype(np.float64), axis, -1)
    blocks = v.reshape(v.shape[:-1] + (-1, 32))
    amax = np.abs(blocks).max(-1, keepdims=True)
    byte = np.maximum(np.where(amax > 0, np.frexp(amax)[1] - 1 + 127, 0) - down, 1)
    scale = np.exp2(byte - 127.0)
    codes = (blocks / scale).astype(np.float32).astype(dtype).astype(np.float64)
    return np.moveaxis((codes * scale).reshape(v.shape), -1, axis)


WIDE = False


def mx_kscale(k):
    if not WIDE:
        return np.ones(k)
    levels = np.array([10, -10, 5, -5, 0])
    if k % 512:
        return np.exp2(np.random.permutation(np.resize(levels, k // 32))).repeat(32)
    a = np.empty((k // 512, 16))
    for p in range(k // 512):
        a[p, :8] = np.random.permutation(np.resize(levels, 8))
        for g in range(8):
            far = levels[np.abs(levels - a[p, g]) >= 10]
            a[p, g + 8] = far[np.random.randint(len(far))]
    return np.exp2(a.ravel()).repeat(32)


BF16 = ml_dtypes.bfloat16


def bf(x):
    return np.asarray(x, np.float32).astype(BF16)


def f64(x):
    return np.asarray(x).astype(np.float64)


E2M1 = np.array([0.0, 0.5, 1.0, 1.5, 2.0, 3.0, 4.0, 6.0, -0.0, -0.5, -1.0, -1.5, -2.0, -3.0, -4.0, -6.0])


def pack_weight(w, fmt):
    k, n = w.shape
    w = f64(bf(w)).reshape(k // 32, 32, n)
    amax = np.abs(w).max(1)
    if fmt == "e4m3":
        byte = np.frexp(amax)[1] - 1 + 127 - 7
    else:
        mant, ex = np.frexp(amax / 6.0)
        byte = np.where(mant > 0.5, ex, ex - 1) + 127
    byte = np.clip(np.where(amax > 0, byte, 1), 1, 254)
    scaled = (w * np.exp2(127.0 - byte)[:, None, :]).reshape(k, n).astype(np.float32)
    by_word = np.ascontiguousarray(scaled.reshape(k // 512, 128, 4, n).transpose(0, 1, 3, 2))
    if fmt == "e4m3":
        words = by_word.astype(ml_dtypes.float8_e4m3fn).view(np.uint8)
    else:
        c = by_word.astype(ml_dtypes.float4_e2m1fn).view(np.uint8) & 0xF
        words = c[..., 0::2] | (c[..., 1::2] << 4)
    return np.ascontiguousarray(words), np.ascontiguousarray(byte.astype(np.uint8).reshape(k // 512, 16, n))


def unpack_weight(words, scales, fmt):
    g, p, n, _ = words.shape
    if fmt == "e4m3":
        vals = np.ascontiguousarray(words).view(ml_dtypes.float8_e4m3fn).astype(np.float64)
    else:
        nib = np.empty((g, p, n, 4), np.uint8)
        nib[..., 0::2] = words & 0xF
        nib[..., 1::2] = words >> 4
        vals = E2M1[nib]
    vals = vals * np.repeat(np.exp2(scales.astype(np.float64) - 127.0), 8, axis=1)[..., None]
    return vals.transpose(0, 1, 3, 2).reshape(g * 512, n)
def pack4(w):
    words, scales = pack_weight(w, "e2m1")
    return words.reshape(words.shape[0], 128, -1), scales


def unpack4(words, scales):
    return unpack_weight(words.reshape(words.shape[0], 128, -1, 2), scales, "e2m1")


def planes(Y):
    n, m = Y.shape
    b = f64(bf(Y)).reshape(n // 32, 32, m)
    amax = np.abs(b).max(1)
    byte = np.clip(np.where(amax > 0, np.frexp(amax)[1] - 1 + 127 - 7, 1), 1, 254)
    codes = (b * np.exp2(127.0 - byte)[:, None, :]).reshape(n, m).astype(np.float32).astype(ml_dtypes.float8_e4m3fn).view(np.uint8)
    words = codes.reshape(n // 512, 128, 4, m).transpose(0, 1, 3, 2)
    return np.ascontiguousarray(words), np.ascontiguousarray(byte.astype(np.uint8).reshape(n // 512, 16, m))


S, K, R, D = 4096, 1024, 512, 1024

def setup_inputs():
    rnd = np.random.randn
    sk = mx_kscale(K)
    t = mx_kscale(S)
    x = 0.25 + rnd(S, K)
    centre = 2.0 / K + 0.4 * rnd(K) / np.sqrt(K)
    treated = np.random.rand(S) < 1.0 / (1.0 + np.exp(-(x * centre).sum(axis=1)))
    sign = np.where(treated, 1.0, -1.0)
    rate = treated.mean()
    numer = np.where(treated, rate, 1.0 - rate)
    outcome = 0.5 + rnd(S)
    coef = centre[:, None] + 0.5 * rnd(K, R) / np.sqrt(K)
    x_words, x_scales = pack4((x * sign[:, None]).T * sk[:, None])
    coef_words, coef_scales = pack4(coef / sk[:, None])
    return {
        "x_words": x_words, "x_scales": x_scales,
        "coef_words": coef_words, "coef_scales": coef_scales,
        "h": bf(numer * outcome * t),
        "cov": bf(rnd(S, D) / np.sqrt(S) / t[:, None]),
        "prior": bf(0.5 * rnd(D)),
        "gain": bf(np.exp(0.8 * rnd(D))),
    }

def reference(x_words, x_scales, coef_words, coef_scales, h, cov, prior, gain):
    XS = unpack4(x_words, x_scales)
    B = unpack4(coef_words, coef_scales)
    L = XS.T @ B
    U = (1.0 + np.exp(-L)) * f64(h)[:, None]
    moment = mxq(U, 0, "e4m3").T @ mxq(f64(cov), 0, "e4m3")
    y = (moment + f64(prior)) * f64(gain)
    Y = y.T
    words, scales = planes(Y)
    return y, words, scales

@@ -1,0 +1,311 @@
+from contextlib import ExitStack
+
+import concourse.mybir as mybir
+from concourse.masks import make_identity
+
+S, K, R, D = 4096, 1024, 512, 1024
+FLOPS = 2 * S * K * R + 2 * S * R * D
+
+F32 = mybir.dt.float32
+BF16 = mybir.dt.bfloat16
+I32 = mybir.dt.int32
+U32 = mybir.dt.uint32
+U8 = mybir.dt.uint8
+FP8X4 = mybir.dt.float8_e4m3fn_x4
+FP4X4 = mybir.dt.float4_e2m1fn_x4
+ACT = mybir.ActivationFunctionType
+ALU = mybir.AluOpType
+
+P = 128
+PACK = 4
+K_PASS = P * PACK
+K_PASSES = K // K_PASS
+S_PASSES = S // K_PASS
+D_GROUPS = D // K_PASS
+R_TILES = R // P
+EARLY_PASSES = 2
+UNITS = K_PASS // 8
+SCALAR_UNITS_A = 48
+SCALAR_UNITS_B = 30
+
+
+def tile_ipw_outcome_moments_k5_kernel(
+    tc, x_words, x_scales, coef_words, coef_scales, h, cov, prior, gain, out_0, out_1, out_2
+):
+    nc = tc.nc
+    with ExitStack() as ctx:
+        keep = ctx.enter_context(tc.tile_pool(name="keep", bufs=1))
+        ring = ctx.enter_context(tc.tile_pool(name="ring", bufs=1))
+        psum = ctx.enter_context(tc.psum_pool(name="psum", bufs=1))
+        ctx.enter_context(tc.manual_schedule())
+
+        def bank(b, shape):
+            return psum.tile(shape, F32, name="bank%d" % b, tag="bank%d" % b)
+
+        coef_codes = keep.tile([P, K_PASSES, 2 * R], U8, name="coef_codes", align_bytes=64)
+        coef_plane = keep.tile([P, K_PASSES, R], U8, name="coef_plane", align_bytes=64)
+        x_raw = [keep.tile([P, K_PASSES, 2 * K_PASS], U8, name="x_raw%d" % g) for g in range(S_PASSES)]
+        early = EARLY_PASSES * K_PASS
+        xs_early = keep.tile([P, K_PASSES, early], U8, name="xs_early")
+        xs_late = keep.tile([P, K_PASSES, S - early], U8, name="xs_late")
+        cov_raw = [keep.tile([P, PACK, D], BF16, name="cov_raw%d" % g) for g in range(S_PASSES)]
+        h_rows = keep.tile([P, K_PASS], BF16, name="h_rows")
+        prior_raw = keep.tile([P, D_GROUPS, PACK], BF16, name="prior_raw")
+        gain_raw = keep.tile([P, D_GROUPS, PACK], BF16, name="gain_raw")
+        ident = keep.tile([P, P], F32, name="ident")
+        warm = keep.tile([P, 1], F32, name="warm")
+        warm_out = keep.tile([P, 1], F32, name="warm_out")
+
+        nc.vector.memset(warm[:], 0.0)
+        nc.vector.memset(xs_early[:].bitcast(I32), 0)
+        nc.vector.memset(coef_plane[:].bitcast(I32), 0)
+        nc.vector.memset(h_rows[:], 0.0)
+        nc.vector.memset(xs_late[:].bitcast(I32), 0)
+        nc.scalar.activation(out=warm_out[:], in_=warm[:], func=ACT.Exp)
+        make_identity(nc, ident[:])
+
+        def load_scale_rows(plane, rows):
+            for q in range(4):
+                nc.sync.dma_start(
+                    out=plane[32 * q : 32 * q + 4, :, :].bitcast(I32),
+                    in_=rows[:, 4 * q : 4 * q + 4, :].rearrange("k r n -> r k n").bitcast(I32),
+                )
+
+        def load_x(g):
+            cols = slice(2 * K_PASS * g, 2 * K_PASS * (g + 1))
+            nc.sync.dma_start(
+                out=x_raw[g][:].bitcast(I32), in_=x_words[:, :, cols].rearrange("k p n -> p k n").bitcast(I32)
+            )
+
+        def load_cov(g):
+            rows = cov[K_PASS * g : K_PASS * (g + 1), :].rearrange("(u t e) d -> e u t d", t=PACK, e=4)
+            for e in range(4):
+                nc.sync.dma_start(out=cov_raw[g][e:P:4, :, :], in_=rows[e])
+
+        nc.sync.dma_start(out=coef_codes[:].bitcast(I32), in_=coef_words.rearrange("k p n -> p k n").bitcast(I32))
+        load_x(0)
+        load_scale_rows(xs_early, x_scales[:, :, :early])
+        load_scale_rows(coef_plane, coef_scales)
+        nc.sync.dma_start(out=h_rows[0:S_PASSES, :], in_=h.rearrange("(g s) -> g s", g=S_PASSES))
+        for g in range(S_PASSES):
+            load_cov(g)
+            if g + 1 == EARLY_PASSES:
+                load_scale_rows(xs_late, x_scales[:, :, early:])
+            if g + 1 < S_PASSES:
+                load_x(g + 1)
+        nc.sync.dma_start(out=prior_raw[:], in_=prior.rearrange("(g p t) -> p g t", p=P, t=PACK))
+        nc.sync.dma_start(out=gain_raw[:], in_=gain.rearrange("(g p t) -> p g t", p=P, t=PACK))
+
+        x_codes, x_plane, logits, expo = {}, {}, {}, {}
+        u_rows, u_words, u_codes, u_plane = {}, {}, {}, {}
+        c_words, c_codes, c_plane, moment = {}, {}, {}, {}
+
+        def sort_x(g):
+            x_codes[g] = ring.tile([P, K_PASSES, 2 * K_PASS], U8, name="x_codes", bufs=3, align_bytes=64)
+            x_plane[g] = ring.tile([P, K_PASSES, K_PASS], U8, name="x_plane", bufs=3, align_bytes=64)
+            nc.vector.tensor_copy(
+                out=x_codes[g][:].bitcast(I32).rearrange("p k (t u w) -> p k u t w", t=PACK, w=2),
+                in_=x_raw[g][:].bitcast(I32).rearrange("p k (u t w) -> p k u t w", t=PACK, w=2),
+            )
+            if g < EARLY_PASSES:
+                src = xs_early[:, :, K_PASS * g : K_PASS * (g + 1)]
+            else:
+                src = xs_late[:, :, K_PASS * g - early : K_PASS * (g + 1) - early]
+            nc.vector.tensor_copy(
+                out=x_plane[g][:].bitcast(I32).rearrange("p k (t u) -> p k u t", t=PACK),
+                in_=src.bitcast(I32).rearrange("p k (u t) -> p k u t", t=PACK),
+            )
+
+        def logit_matmuls(g, t):
+            logits[g, t] = bank(4 + t, [P, R])
+            for k in range(K_PASSES):
+                nc.tensor.matmul_mx(
+                    out=logits[g, t][:],
+                    lhsT=x_codes[g][:, k, 2 * P * t : 2 * P * (t + 1)].bitcast(FP4X4),
+                    lhsT_scale=x_plane[g][:, k, P * t : P * (t + 1)],
+                    rhs=coef_codes[:, k, :].bitcast(FP4X4),
+                    rhs_scale=coef_plane[:, k, :],
+                    start=(k == 0),
+                    stop=(k == K_PASSES - 1),
+                )
+
+        def exp_slot(g, t):
+            expo[g, t] = ring.tile([P, R], F32, name="expo", bufs=8)
+            nc.scalar.activation(out=expo[g, t][:], in_=logits[g, t][:], func=ACT.Exp, scale=-1.0)
+
+        def weight_rows(g):
+            u_rows[g] = ring.tile([P, PACK, R], BF16, name="u_rows", bufs=2)
+            for t in range(PACK):
+                nc.vector.tensor_scalar(
+                    out=u_rows[g][:, t, :], in0=expo[g, t][:], scalar1=1.0, scalar2=h_cols[:, t, g : g + 1],
+                    op0=ALU.add, op1=ALU.mult,
+                )
+
+        def interleave_u(g):
+            u_words[g] = ring.tile([P, R * PACK], BF16, name="u_words", bufs=2, align_bytes=64)
+            nc.vector.tensor_copy(
+                out=u_words[g][:].rearrange("p (c i t) -> p c t i", i=4, t=PACK),
+                in_=u_rows[g][:].rearrange("p t (c i) -> p c t i", i=4),
+            )
+
+        def quantise_u(g):
+            u_codes[g] = keep.tile([P, R], U32, name="u_codes%d" % g, align_bytes=64)
+            u_plane[g] = keep.tile([P, R], U8, name="u_plane%d" % g, align_bytes=64)
+            nc.vector.quantize_mx(out=u_codes[g][:].bitcast(FP8X4), scales=u_plane[g][:], in_=u_words[g][:])
+
+        def cov_views(g, dg):
+            if (g, dg) not in c_words:
+                c_words[g, dg] = ring.tile([P, K_PASS * PACK], BF16, name="c_words", bufs=3, align_bytes=64)
+            dst = c_words[g, dg][:].rearrange("p (s n m t) -> p n t m s", s=PACK, m=2, t=PACK)
+            src = cov_raw[g][:, :, K_PASS * dg : K_PASS * (dg + 1)].rearrange("p t (n m s) -> p n t m s", m=2, s=PACK)
+            return dst, src
+
+        def interleave_cov_scalar(g, dg, units):
+            dst, src = cov_views(g, dg)
+            nc.scalar.copy(out=dst[:, :units], in_=src[:, :units])
+
+        def interleave_cov_vector(g, dg, units):
+            dst, src = cov_views(g, dg)
+            nc.vector.tensor_copy(out=dst[:, units:], in_=src[:, units:])
+
+        def quantise_cov(g, dg):
+            c_codes[g, dg] = ring.tile([P, K_PASS], U32, name="c_codes", bufs=5, align_bytes=64)
+            c_plane[g, dg] = ring.tile([P, K_PASS], U8, name="c_plane", bufs=5, align_bytes=64)
+            nc.vector.quantize_mx(
+                out=c_codes[g, dg][:].bitcast(FP8X4), scales=c_plane[g, dg][:], in_=c_words[g, dg][:]
+            )
+
+        def moment_matmuls(g, dg):
+            for s in range(PACK):
+                if g == 0:
+                    moment[dg, s] = bank(4 * dg + s, [P, R])
+                nc.tensor.matmul_mx(
+                    out=moment[dg, s][:],
+                    lhsT=c_codes[g, dg][:, P * s : P * (s + 1)].bitcast(FP8X4),
+                    lhsT_scale=c_plane[g, dg][:, P * s : P * (s + 1)],
+                    rhs=u_codes[g][:].bitcast(FP8X4),
+                    rhs_scale=u_plane[g][:],
+                    start=(g == 0),
+                    stop=(g == S_PASSES - 1),
+                )
+
+        y_rows, y_turned, y_words = {}, {}, {}
+
+        def finish_slot(dg, s, on_scalar):
+            if s == 0:
+                y_rows[dg] = keep.tile([P, PACK, R], F32, name="y_rows%d" % dg)
+            if on_scalar:
+                nc.scalar.activation(
+                    out=y_rows[dg][:, s, :], in_=moment[dg, s][:], func=ACT.Identity,
+                    scale=gain_cols[:, dg, s : s + 1], bias=shift_cols[:, dg, s : s + 1],
+                )
+            else:
+                nc.vector.tensor_scalar(
+                    out=y_rows[dg][:, s, :], in0=moment[dg, s][:], scalar1=gain_cols[:, dg, s : s + 1],
+                    scalar2=shift_cols[:, dg, s : s + 1], op0=ALU.mult, op1=ALU.add,
+                )
+
+        def turn_y(dg, rt):
+            y_turned[dg, rt] = bank(rt, [P, PACK, P])
+            for s in range(PACK):
+                nc.tensor.transpose(y_turned[dg, rt][:, s, :], y_rows[dg][:, s, P * rt : P * (rt + 1)], ident[:])
+
+        def store_y(dg, rt, on_scalar):
+            y_out = ring.tile([P, K_PASS], F32, name="y_out", bufs=8)
+            dst = y_out[:].rearrange("p (m s) -> p m s", s=PACK)
+            src = y_turned[dg, rt][:].rearrange("p s m -> p m s")
+            if on_scalar:
+                nc.scalar.copy(out=dst, in_=src)
+            else:
+                nc.vector.tensor_copy(out=dst, in_=src)
+            nc.sync.dma_start(out=out_0[P * rt : P * (rt + 1), K_PASS * dg : K_PASS * (dg + 1)], in_=y_out[:])
+
+        def interleave_y(dg):
+            y_words[dg] = ring.tile([P, R * PACK], BF16, name="y_words", bufs=2, align_bytes=64)
+            nc.vector.tensor_copy(
+                out=y_words[dg][:].rearrange("p (c i s) -> p c s i", i=4, s=PACK),
+                in_=y_rows[dg][:].rearrange("p s (c i) -> p c s i", i=4),
+            )
+
+        def store_planes(dg):
+            y_codes = keep.tile([P, R], U32, name="y_codes%d" % dg, align_bytes=64)
+            y_plane = keep.tile([P, R], U8, name="y_plane%d" % dg, align_bytes=64)
+            nc.vector.quantize_mx(out=y_codes[:].bitcast(FP8X4), scales=y_plane[:], in_=y_words[dg][:])
+            nc.sync.dma_start(
+                out=out_1[dg].rearrange("p m t -> p (m t)").bitcast(I32), in_=y_codes[:].bitcast(I32)
+            )
+            for q in range(4):
+                nc.sync.dma_start(
+                    out=out_2[dg, 4 * q : 4 * q + 4, :].bitcast(I32),
+                    in_=y_plane[32 * q : 32 * q + 4, :].bitcast(I32),
+                )
+
+        sort_x(0)
+        h_sorted = keep.tile([P, PACK, P], F32, name="h_sorted")
+        nc.scalar.copy(
+            out=h_sorted[:].rearrange("p t (u e) -> p t u e", e=4),
+            in_=h_rows[:].rearrange("p (u t e) -> p t u e", t=PACK, e=4),
+        )
+        for t in range(PACK):
+            logit_matmuls(0, t)
+        h_turned = bank(0, [P, PACK, P])
+        for t in range(PACK):
+            nc.tensor.transpose(h_turned[:, t, :], h_sorted[:, t, :], ident[:])
+        interleave_cov_vector(0, 0, 0)
+        sort_x(1)
+        quantise_cov(0, 0)
+        h_cols = keep.tile([P, PACK, S_PASSES], F32, name="h_cols")
+        nc.vector.tensor_copy(out=h_cols[:], in_=h_turned[:, :, 0:S_PASSES])
+
+        pieces = [(g, dg) for dg in range(D_GROUPS) for g in range(S_PASSES)]
+        for g in range(S_PASSES):
+            piece = pieces[g + 1]
+            for t in range(PACK):
+                exp_slot(g, t)
+                if g + 1 < S_PASSES:
+                    logit_matmuls(g + 1, t)
+            if g >= 1:
+                moment_matmuls(g - 1, 0)
+            interleave_cov_scalar(*piece, SCALAR_UNITS_A)
+            weight_rows(g)
+            interleave_cov_vector(*piece, SCALAR_UNITS_A)
+            interleave_u(g)
+            if g + 2 < S_PASSES:
+                sort_x(g + 2)
+            quantise_cov(*piece)
+            quantise_u(g)
+
+        gain_cols = keep.tile([P, D_GROUPS, PACK], F32, name="gain_cols")
+        shift_cols = keep.tile([P, D_GROUPS, PACK], F32, name="shift_cols")
+        nc.vector.tensor_copy(out=gain_cols[:], in_=gain_raw[:])
+        nc.vector.tensor_tensor(out=shift_cols[:], in0=prior_raw[:], in1=gain_raw[:], op=ALU.mult)
+
+        moment_matmuls(0, 1)
+        moment_matmuls(S_PASSES - 1, 0)
+        interleave_cov_scalar(1, 1, SCALAR_UNITS_B)
+        interleave_cov_vector(1, 1, SCALAR_UNITS_B)
+        for g in range(1, S_PASSES):
+            if g + 1 < S_PASSES:
+                interleave_cov_scalar(g + 1, 1, SCALAR_UNITS_B)
+                interleave_cov_vector(g + 1, 1, SCALAR_UNITS_B)
+            quantise_cov(g, 1)
+            moment_matmuls(g, 1)
+            if g <= PACK:
+                finish_slot(0, g - 1, True)
+            if g == PACK + 1:
+                for rt in range(R_TILES):
+                    turn_y(0, rt)
+        interleave_y(0)
+        for rt in range(R_TILES):
+            store_y(0, rt, True)
+        store_planes(0)
+        for s in range(PACK):
+            finish_slot(1, s, s % 2 == 1)
+        for rt in range(R_TILES):
+            turn_y(1, rt)
+        interleave_y(1)
+        store_y(1, 0, True)
+        store_y(1, 1, True)
+        store_planes(1)
+        store_y(1, 2, True)
+        store_y(1, 3, False)

@@ -23,10 +23,19 @@ K_PASSES = K // K_PASS
 S_PASSES = S // K_PASS
 D_GROUPS = D // K_PASS
 R_TILES = R // P
-EARLY_PASSES = 2
+EARLY_PASSES = 3
 UNITS = K_PASS // 8
-SCALAR_UNITS_A = 48
-SCALAR_UNITS_B = 30
+SCALAR_UNITS = 26
+HEAD = 0
+FIRST_ON_SCALAR = 2
+COEF_Q = 0
+LAG = 2
+HEAD_UNITS = 24
+XFIRST = 0
+TAIL = 0
+PL0 = 7
+S_EVEN = 3
+S_ODD = 4
 
 
 def tile_ipw_outcome_moments_k5_kernel(
@@ -48,7 +57,7 @@ def tile_ipw_outcome_moments_k5_kernel(
         early = EARLY_PASSES * K_PASS
         xs_early = keep.tile([P, K_PASSES, early], U8, name="xs_early")
         xs_late = keep.tile([P, K_PASSES, S - early], U8, name="xs_late")
-        cov_raw = [keep.tile([P, PACK, D], BF16, name="cov_raw%d" % g) for g in range(S_PASSES)]
+        cov_raw = {}
         h_rows = keep.tile([P, K_PASS], BF16, name="h_rows")
         prior_raw = keep.tile([P, D_GROUPS, PACK], BF16, name="prior_raw")
         gain_raw = keep.tile([P, D_GROUPS, PACK], BF16, name="gain_raw")
@@ -57,16 +66,16 @@ def tile_ipw_outcome_moments_k5_kernel(
         warm_out = keep.tile([P, 1], F32, name="warm_out")
 
         nc.vector.memset(warm[:], 0.0)
+        nc.vector.memset(h_rows[:], 0.0)
         nc.vector.memset(xs_early[:].bitcast(I32), 0)
         nc.vector.memset(coef_plane[:].bitcast(I32), 0)
-        nc.vector.memset(h_rows[:], 0.0)
         nc.vector.memset(xs_late[:].bitcast(I32), 0)
         nc.scalar.activation(out=warm_out[:], in_=warm[:], func=ACT.Exp)
         make_identity(nc, ident[:])
 
-        def load_scale_rows(plane, rows):
+        def load_scale_rows(plane, rows, queue):
             for q in range(4):
-                nc.sync.dma_start(
+                queue.dma_start(
                     out=plane[32 * q : 32 * q + 4, :, :].bitcast(I32),
                     in_=rows[:, 4 * q : 4 * q + 4, :].rearrange("k r n -> r k n").bitcast(I32),
                 )
@@ -77,24 +86,38 @@ def tile_ipw_outcome_moments_k5_kernel(
                 out=x_raw[g][:].bitcast(I32), in_=x_words[:, :, cols].rearrange("k p n -> p k n").bitcast(I32)
             )
 
-        def load_cov(g):
-            rows = cov[K_PASS * g : K_PASS * (g + 1), :].rearrange("(u t e) d -> e u t d", t=PACK, e=4)
+        def load_cov_rows(dst, g, cols):
+            rows = cov[K_PASS * g : K_PASS * (g + 1), cols].rearrange("(u t e) d -> e u t d", t=PACK, e=4)
             for e in range(4):
-                nc.sync.dma_start(out=cov_raw[g][e:P:4, :, :], in_=rows[e])
+                nc.sync.dma_start(out=dst[e:P:4, :, :], in_=rows[e])
+
+        def load_cov(g, dg):
+            piece = keep.tile([P, PACK, K_PASS], BF16, name="cov_raw%d_%d" % (g, dg))
+            load_cov_rows(piece, g, slice(K_PASS * dg, K_PASS * (dg + 1)))
+            cov_raw[g, dg] = piece[:]
 
         nc.sync.dma_start(out=coef_codes[:].bitcast(I32), in_=coef_words.rearrange("k p n -> p k n").bitcast(I32))
         load_x(0)
-        load_scale_rows(xs_early, x_scales[:, :, :early])
-        load_scale_rows(coef_plane, coef_scales)
         nc.sync.dma_start(out=h_rows[0:S_PASSES, :], in_=h.rearrange("(g s) -> g s", g=S_PASSES))
-        for g in range(S_PASSES):
-            load_cov(g)
+        load_scale_rows(xs_early, x_scales[:, :, :early], nc.sync)
+        load_scale_rows(coef_plane, coef_scales, nc.gpsimd if COEF_Q else nc.sync)
+        if HEAD == 0:
+            load_cov(0, 0)
+        load_x(1)
+        if HEAD == 1:
+            load_cov(0, 0)
+        for g in range(1, S_PASSES):
+            if XFIRST and g + 1 < S_PASSES:
+                load_x(g + 1)
+            load_cov(g, 0)
             if g + 1 == EARLY_PASSES:
-                load_scale_rows(xs_late, x_scales[:, :, early:])
-            if g + 1 < S_PASSES:
+                load_scale_rows(xs_late, x_scales[:, :, early:], nc.sync)
+            if not XFIRST and g + 1 < S_PASSES:
                 load_x(g + 1)
         nc.sync.dma_start(out=prior_raw[:], in_=prior.rearrange("(g p t) -> p g t", p=P, t=PACK))
         nc.sync.dma_start(out=gain_raw[:], in_=gain.rearrange("(g p t) -> p g t", p=P, t=PACK))
+        for g in range(S_PASSES):
+            load_cov(g, 1)
 
         x_codes, x_plane, logits, expo = {}, {}, {}, {}
         u_rows, u_words, u_codes, u_plane = {}, {}, {}, {}
@@ -130,15 +153,21 @@ def tile_ipw_outcome_moments_k5_kernel(
                 )
 
         def exp_slot(g, t):
-            expo[g, t] = ring.tile([P, R], F32, name="expo", bufs=8)
+            expo[g, t] = ring.tile([P, R], F32, name="expo", bufs=6)
             nc.scalar.activation(out=expo[g, t][:], in_=logits[g, t][:], func=ACT.Exp, scale=-1.0)
 
-        def weight_rows(g):
-            u_rows[g] = ring.tile([P, PACK, R], BF16, name="u_rows", bufs=2)
-            for t in range(PACK):
+        def weight_slot(g, t, on_scalar):
+            if g not in u_rows:
+                u_rows[g] = ring.tile([P, PACK, R], BF16, name="u_rows", bufs=3)
+            h_col = h_cols[:, t, g : g + 1]
+            if on_scalar:
+                nc.scalar.activation(
+                    out=u_rows[g][:, t, :], in_=expo[g, t][:], func=ACT.Identity, scale=h_col, bias=h_col
+                )
+            else:
                 nc.vector.tensor_scalar(
-                    out=u_rows[g][:, t, :], in0=expo[g, t][:], scalar1=1.0, scalar2=h_cols[:, t, g : g + 1],
-                    op0=ALU.add, op1=ALU.mult,
+                    out=u_rows[g][:, t, :], in0=expo[g, t][:], scalar1=h_col, scalar2=h_col,
+                    op0=ALU.mult, op1=ALU.add,
                 )
 
         def interleave_u(g):
@@ -157,7 +186,7 @@ def tile_ipw_outcome_moments_k5_kernel(
             if (g, dg) not in c_words:
                 c_words[g, dg] = ring.tile([P, K_PASS * PACK], BF16, name="c_words", bufs=3, align_bytes=64)
             dst = c_words[g, dg][:].rearrange("p (s n m t) -> p n t m s", s=PACK, m=2, t=PACK)
-            src = cov_raw[g][:, :, K_PASS * dg : K_PASS * (dg + 1)].rearrange("p t (n m s) -> p n t m s", m=2, s=PACK)
+            src = cov_raw[g, dg].rearrange("p t (n m s) -> p n t m s", m=2, s=PACK)
             return dst, src
 
         def interleave_cov_scalar(g, dg, units):
@@ -169,8 +198,8 @@ def tile_ipw_outcome_moments_k5_kernel(
             nc.vector.tensor_copy(out=dst[:, units:], in_=src[:, units:])
 
         def quantise_cov(g, dg):
-            c_codes[g, dg] = ring.tile([P, K_PASS], U32, name="c_codes", bufs=5, align_bytes=64)
-            c_plane[g, dg] = ring.tile([P, K_PASS], U8, name="c_plane", bufs=5, align_bytes=64)
+            c_codes[g, dg] = ring.tile([P, K_PASS], U32, name="c_codes%d" % dg, bufs=5, align_bytes=64)
+            c_plane[g, dg] = ring.tile([P, K_PASS], U8, name="c_plane%d" % dg, bufs=5, align_bytes=64)
             nc.vector.quantize_mx(
                 out=c_codes[g, dg][:].bitcast(FP8X4), scales=c_plane[g, dg][:], in_=c_words[g, dg][:]
             )
@@ -191,17 +220,17 @@ def tile_ipw_outcome_moments_k5_kernel(
 
         y_rows, y_turned, y_words = {}, {}, {}
 
-        def finish_slot(dg, s, on_scalar):
-            if s == 0:
+        def finish_slot(dg, s, cols, on_scalar):
+            if dg not in y_rows:
                 y_rows[dg] = keep.tile([P, PACK, R], F32, name="y_rows%d" % dg)
             if on_scalar:
                 nc.scalar.activation(
-                    out=y_rows[dg][:, s, :], in_=moment[dg, s][:], func=ACT.Identity,
+                    out=y_rows[dg][:, s, cols], in_=moment[dg, s][:, cols], func=ACT.Identity,
                     scale=gain_cols[:, dg, s : s + 1], bias=shift_cols[:, dg, s : s + 1],
                 )
             else:
                 nc.vector.tensor_scalar(
-                    out=y_rows[dg][:, s, :], in0=moment[dg, s][:], scalar1=gain_cols[:, dg, s : s + 1],
+                    out=y_rows[dg][:, s, cols], in0=moment[dg, s][:, cols], scalar1=gain_cols[:, dg, s : s + 1],
                     scalar2=shift_cols[:, dg, s : s + 1], op0=ALU.mult, op1=ALU.add,
                 )
 
@@ -211,7 +240,7 @@ def tile_ipw_outcome_moments_k5_kernel(
                 nc.tensor.transpose(y_turned[dg, rt][:, s, :], y_rows[dg][:, s, P * rt : P * (rt + 1)], ident[:])
 
         def store_y(dg, rt, on_scalar):
-            y_out = ring.tile([P, K_PASS], F32, name="y_out", bufs=8)
+            y_out = ring.tile([P, K_PASS], F32, name="y_out", bufs=6)
             dst = y_out[:].rearrange("p (m s) -> p m s", s=PACK)
             src = y_turned[dg, rt][:].rearrange("p s m -> p m s")
             if on_scalar:
@@ -220,14 +249,14 @@ def tile_ipw_outcome_moments_k5_kernel(
                 nc.vector.tensor_copy(out=dst, in_=src)
             nc.sync.dma_start(out=out_0[P * rt : P * (rt + 1), K_PASS * dg : K_PASS * (dg + 1)], in_=y_out[:])
 
-        def interleave_y(dg):
+        def interleave_y(dg, cols):
             y_words[dg] = ring.tile([P, R * PACK], BF16, name="y_words", bufs=2, align_bytes=64)
             nc.vector.tensor_copy(
                 out=y_words[dg][:].rearrange("p (c i s) -> p c s i", i=4, s=PACK),
                 in_=y_rows[dg][:].rearrange("p s (c i) -> p c s i", i=4),
             )
 
-        def store_planes(dg):
+        def store_planes(dg, cols):
             y_codes = keep.tile([P, R], U32, name="y_codes%d" % dg, align_bytes=64)
             y_plane = keep.tile([P, R], U8, name="y_plane%d" % dg, align_bytes=64)
             nc.vector.quantize_mx(out=y_codes[:].bitcast(FP8X4), scales=y_plane[:], in_=y_words[dg][:])
@@ -240,72 +269,99 @@ def tile_ipw_outcome_moments_k5_kernel(
                     in_=y_plane[32 * q : 32 * q + 4, :].bitcast(I32),
                 )
 
-        sort_x(0)
         h_sorted = keep.tile([P, PACK, P], F32, name="h_sorted")
         nc.scalar.copy(
             out=h_sorted[:].rearrange("p t (u e) -> p t u e", e=4),
             in_=h_rows[:].rearrange("p (u t e) -> p t u e", t=PACK, e=4),
         )
-        for t in range(PACK):
-            logit_matmuls(0, t)
         h_turned = bank(0, [P, PACK, P])
         for t in range(PACK):
             nc.tensor.transpose(h_turned[:, t, :], h_sorted[:, t, :], ident[:])
-        interleave_cov_vector(0, 0, 0)
-        sort_x(1)
-        quantise_cov(0, 0)
         h_cols = keep.tile([P, PACK, S_PASSES], F32, name="h_cols")
-        nc.vector.tensor_copy(out=h_cols[:], in_=h_turned[:, :, 0:S_PASSES])
+        nc.scalar.copy(out=h_cols[:], in_=h_turned[:, :, 0:S_PASSES])
+        sort_x(0)
+        for t in range(PACK):
+            logit_matmuls(0, t)
+        if HEAD == 0:
+            interleave_cov_vector(0, 0, 0)
+            sort_x(1)
+        else:
+            sort_x(1)
+            interleave_cov_vector(0, 0, 0)
 
         pieces = [(g, dg) for dg in range(D_GROUPS) for g in range(S_PASSES)]
         for g in range(S_PASSES):
-            piece = pieces[g + 1]
+            on_scalar = FIRST_ON_SCALAR if g == 0 else (S_EVEN if g % 2 == 0 else S_ODD)
+            interleave_cov_vector(*pieces[g + 1], 0)
+            if g >= 1:
+                quantise_u(g - 1)
+            else:
+                quantise_cov(0, 0)
+            if g + 2 < S_PASSES:
+                sort_x(g + 2)
+            quantise_cov(*pieces[g + 1])
             for t in range(PACK):
                 exp_slot(g, t)
                 if g + 1 < S_PASSES:
                     logit_matmuls(g + 1, t)
-            if g >= 1:
-                moment_matmuls(g - 1, 0)
-            interleave_cov_scalar(*piece, SCALAR_UNITS_A)
-            weight_rows(g)
-            interleave_cov_vector(*piece, SCALAR_UNITS_A)
+                if t >= 1:
+                    weight_slot(g, t - 1, t - 1 >= PACK - on_scalar)
+            if g >= LAG:
+                moment_matmuls(g - LAG, 0)
+            weight_slot(g, PACK - 1, on_scalar > 0)
             interleave_u(g)
-            if g + 2 < S_PASSES:
-                sort_x(g + 2)
-            quantise_cov(*piece)
-            quantise_u(g)
 
         gain_cols = keep.tile([P, D_GROUPS, PACK], F32, name="gain_cols")
         shift_cols = keep.tile([P, D_GROUPS, PACK], F32, name="shift_cols")
+
+        for g in range(S_PASSES - LAG, S_PASSES - 1):
+            moment_matmuls(g, 0)
+        moment_matmuls(0, 1)
+        interleave_cov_scalar(1, 1, SCALAR_UNITS)
+        interleave_cov_vector(1, 1, SCALAR_UNITS)
+        quantise_u(S_PASSES - 1)
+        moment_matmuls(S_PASSES - 1, 0)
         nc.vector.tensor_copy(out=gain_cols[:], in_=gain_raw[:])
         nc.vector.tensor_tensor(out=shift_cols[:], in0=prior_raw[:], in1=gain_raw[:], op=ALU.mult)
-
-        moment_matmuls(0, 1)
-        moment_matmuls(S_PASSES - 1, 0)
-        interleave_cov_scalar(1, 1, SCALAR_UNITS_B)
-        interleave_cov_vector(1, 1, SCALAR_UNITS_B)
+        whole = slice(0, R)
         for g in range(1, S_PASSES):
             if g + 1 < S_PASSES:
-                interleave_cov_scalar(g + 1, 1, SCALAR_UNITS_B)
-                interleave_cov_vector(g + 1, 1, SCALAR_UNITS_B)
+                interleave_cov_scalar(g + 1, 1, SCALAR_UNITS)
+                interleave_cov_vector(g + 1, 1, SCALAR_UNITS)
+            if g == PL0 or (PL0 == 16 and g == 6):
+                interleave_y(0, whole)
             quantise_cov(g, 1)
+            if g == PL0 or (PL0 == 16 and g == 7):
+                store_planes(0, whole)
             moment_matmuls(g, 1)
-            if g <= PACK:
-                finish_slot(0, g - 1, True)
-            if g == PACK + 1:
+            if 1 <= g < 3:
+                finish_slot(0, 2 * g - 2, whole, True)
+                finish_slot(0, 2 * g - 1, whole, True)
+            if g == 3:
                 for rt in range(R_TILES):
                     turn_y(0, rt)
-        interleave_y(0)
-        for rt in range(R_TILES):
-            store_y(0, rt, True)
-        store_planes(0)
-        for s in range(PACK):
-            finish_slot(1, s, s % 2 == 1)
-        for rt in range(R_TILES):
-            turn_y(1, rt)
-        interleave_y(1)
-        store_y(1, 0, True)
-        store_y(1, 1, True)
-        store_planes(1)
-        store_y(1, 2, True)
-        store_y(1, 3, False)
+            if g >= 4:
+                store_y(0, g - 4, True)
+        if PL0 == 8:
+            interleave_y(0, whole)
+            store_planes(0, whole)
+        halves = [slice(0, R // 2), slice(R // 2, R)]
+        for half in range(2):
+            for s in range(PACK):
+                finish_slot(1, s, halves[half], s % 2 == 0)
+            for rt in range(2 * half, 2 * half + 2):
+                turn_y(1, rt)
+        if TAIL == 0:
+            store_y(1, 0, True)
+            interleave_y(1, whole)
+            store_y(1, 1, True)
+            store_y(1, 2, True)
+            store_planes(1, whole)
+            store_y(1, 3, True)
+        if TAIL == 1:
+            store_y(1, 0, True)
+            store_y(1, 1, False)
+            interleave_y(1, whole)
+            store_y(1, 2, True)
+            store_y(1, 3, True)
+            store_planes(1, whole)

@@ -25,11 +25,18 @@ D_GROUPS = D // K_PASS
 R_TILES = R // P
 EARLY_PASSES = 3
 UNITS = K_PASS // 8
-SCALAR_UNITS = 26
+SCALAR_UNITS = 22
 HEAD = 0
 FIRST_ON_SCALAR = 2
 COEF_Q = 0
 LAG = 2
+UNITS_A = 34
+LB = 3
+SU_FIRST = 32
+FIN = 3
+SPLIT = 0
+TURN = 4
+CB = 2
 HEAD_UNITS = 24
 XFIRST = 0
 TAIL = 0
@@ -104,8 +111,6 @@ def tile_ipw_outcome_moments_k5_kernel(
         if HEAD == 0:
             load_cov(0, 0)
         load_x(1)
-        if HEAD == 1:
-            load_cov(0, 0)
         for g in range(1, S_PASSES):
             if XFIRST and g + 1 < S_PASSES:
                 load_x(g + 1)
@@ -139,42 +144,33 @@ def tile_ipw_outcome_moments_k5_kernel(
                 in_=src.bitcast(I32).rearrange("p k (u t) -> p k u t", t=PACK),
             )
 
-        def logit_matmuls(g, t):
-            logits[g, t] = bank(4 + t, [P, R])
-            for k in range(K_PASSES):
-                nc.tensor.matmul_mx(
-                    out=logits[g, t][:],
-                    lhsT=x_codes[g][:, k, 2 * P * t : 2 * P * (t + 1)].bitcast(FP4X4),
-                    lhsT_scale=x_plane[g][:, k, P * t : P * (t + 1)],
-                    rhs=coef_codes[:, k, :].bitcast(FP4X4),
-                    rhs_scale=coef_plane[:, k, :],
-                    start=(k == 0),
-                    stop=(k == K_PASSES - 1),
-                )
+        def logit_matmuls(g, rt):
+            logits[g, rt] = bank(8 - LB + (R_TILES * g + rt) % LB, [P, PACK, P])
+            for t in range(PACK):
+                for k in range(K_PASSES):
+                    nc.tensor.matmul_mx(
+                        out=logits[g, rt][:, t, :],
+                        lhsT=x_codes[g][:, k, 2 * P * t : 2 * P * (t + 1)].bitcast(FP4X4),
+                        lhsT_scale=x_plane[g][:, k, P * t : P * (t + 1)],
+                        rhs=coef_codes[:, k, 2 * P * rt : 2 * P * (rt + 1)].bitcast(FP4X4),
+                        rhs_scale=coef_plane[:, k, P * rt : P * (rt + 1)],
+                        start=(k == 0),
+                        stop=(k == K_PASSES - 1),
+                    )
 
-        def exp_slot(g, t):
-            expo[g, t] = ring.tile([P, R], F32, name="expo", bufs=6)
-            nc.scalar.activation(out=expo[g, t][:], in_=logits[g, t][:], func=ACT.Exp, scale=-1.0)
+        def exp_tile(g, rt):
+            if rt == 0:
+                expo[g] = ring.tile([P, R, PACK], F32, name="expo", bufs=2)
+            nc.scalar.activation(
+                out=expo[g][:, P * rt : P * (rt + 1), :], in_=logits[g, rt][:].rearrange("p t r -> p r t"),
+                func=ACT.Exp, scale=-1.0,
+            )
 
-        def weight_slot(g, t, on_scalar):
-            if g not in u_rows:
-                u_rows[g] = ring.tile([P, PACK, R], BF16, name="u_rows", bufs=3)
-            h_col = h_cols[:, t, g : g + 1]
-            if on_scalar:
-                nc.scalar.activation(
-                    out=u_rows[g][:, t, :], in_=expo[g, t][:], func=ACT.Identity, scale=h_col, bias=h_col
-                )
-            else:
-                nc.vector.tensor_scalar(
-                    out=u_rows[g][:, t, :], in0=expo[g, t][:], scalar1=h_col, scalar2=h_col,
-                    op0=ALU.mult, op1=ALU.add,
-                )
-
-        def interleave_u(g):
+        def weight_u(g):
             u_words[g] = ring.tile([P, R * PACK], BF16, name="u_words", bufs=2, align_bytes=64)
-            nc.vector.tensor_copy(
-                out=u_words[g][:].rearrange("p (c i t) -> p c t i", i=4, t=PACK),
-                in_=u_rows[g][:].rearrange("p t (c i) -> p c t i", i=4),
+            nc.vector.scalar_tensor_tensor(
+                out=u_words[g][:].rearrange("p (r t) -> p r t", t=PACK), in0=expo[g][:], scalar=1.0,
+                in1=h_turned[:, g : g + 1, :].to_broadcast([P, R, PACK]), op0=ALU.add, op1=ALU.mult,
             )
 
         def quantise_u(g):
@@ -182,9 +178,20 @@ def tile_ipw_outcome_moments_k5_kernel(
             u_plane[g] = keep.tile([P, R], U8, name="u_plane%d" % g, align_bytes=64)
             nc.vector.quantize_mx(out=u_codes[g][:].bitcast(FP8X4), scales=u_plane[g][:], in_=u_words[g][:])
 
+        def new_cov_words(g, dg, name, bufs):
+            c_words[g, dg] = ring.tile([P, K_PASS * PACK], BF16, name=name, bufs=bufs, align_bytes=64)
+
+        def interleave_cov_gpsimd(g, dg, units):
+            dst = c_words[g, dg][:].rearrange("p (s m t) -> p s m t", s=PACK, t=PACK)
+            src = cov_raw[g, dg].rearrange("p t (m s) -> p s m t", s=PACK)
+            nc.gpsimd.tensor_scalar(
+                out=dst[:, :, 2 * units :, :], in0=src[:, :, 2 * units :, :], scalar1=1.0, scalar2=0.0,
+                op0=ALU.mult, op1=ALU.add,
+            )
+
         def cov_views(g, dg):
             if (g, dg) not in c_words:
-                c_words[g, dg] = ring.tile([P, K_PASS * PACK], BF16, name="c_words", bufs=3, align_bytes=64)
+                new_cov_words(g, dg, "c_words", 3)
             dst = c_words[g, dg][:].rearrange("p (s n m t) -> p n t m s", s=PACK, m=2, t=PACK)
             src = cov_raw[g, dg].rearrange("p t (n m s) -> p n t m s", m=2, s=PACK)
             return dst, src
@@ -274,74 +281,73 @@ def tile_ipw_outcome_moments_k5_kernel(
             out=h_sorted[:].rearrange("p t (u e) -> p t u e", e=4),
             in_=h_rows[:].rearrange("p (u t e) -> p t u e", t=PACK, e=4),
         )
-        h_turned = bank(0, [P, PACK, P])
+        h_turned = bank(4, [P, P, PACK])
         for t in range(PACK):
-            nc.tensor.transpose(h_turned[:, t, :], h_sorted[:, t, :], ident[:])
-        h_cols = keep.tile([P, PACK, S_PASSES], F32, name="h_cols")
-        nc.scalar.copy(out=h_cols[:], in_=h_turned[:, :, 0:S_PASSES])
+            nc.tensor.transpose(h_turned[:, :, t], h_sorted[:, t, :], ident[:])
         sort_x(0)
-        for t in range(PACK):
-            logit_matmuls(0, t)
-        if HEAD == 0:
-            interleave_cov_vector(0, 0, 0)
-            sort_x(1)
-        else:
-            sort_x(1)
-            interleave_cov_vector(0, 0, 0)
-
+        for rt in range(LB):
+            logit_matmuls(0, rt)
+        new_cov_words(0, 0, "c_shared", CB)
+        interleave_cov_vector(0, 0, 0)
+        sort_x(1)
         pieces = [(g, dg) for dg in range(D_GROUPS) for g in range(S_PASSES)]
+        new_cov_words(1, 0, "c_shared", CB)
+        interleave_cov_vector(1, 0, 0)
+
         for g in range(S_PASSES):
-            on_scalar = FIRST_ON_SCALAR if g == 0 else (S_EVEN if g % 2 == 0 else S_ODD)
-            interleave_cov_vector(*pieces[g + 1], 0)
-            if g >= 1:
-                quantise_u(g - 1)
-            else:
-                quantise_cov(0, 0)
-            if g + 2 < S_PASSES:
-                sort_x(g + 2)
-            quantise_cov(*pieces[g + 1])
-            for t in range(PACK):
-                exp_slot(g, t)
-                if g + 1 < S_PASSES:
-                    logit_matmuls(g + 1, t)
-                if t >= 1:
-                    weight_slot(g, t - 1, t - 1 >= PACK - on_scalar)
+            for rt in range(R_TILES):
+                exp_tile(g, rt)
+                ahead = R_TILES * g + rt + LB
+                if ahead < R_TILES * S_PASSES:
+                    logit_matmuls(ahead // R_TILES, ahead % R_TILES)
             if g >= LAG:
                 moment_matmuls(g - LAG, 0)
-            weight_slot(g, PACK - 1, on_scalar > 0)
-            interleave_u(g)
+            quantise_cov(g, 0)
+            new_cov_words(*pieces[g + 2], "c_shared", CB)
+            weight_u(g)
+            interleave_cov_gpsimd(*pieces[g + 2], UNITS_A)
+            if g >= 1:
+                interleave_cov_scalar(*pieces[g + 1], UNITS_A)
+            if g + 2 < S_PASSES:
+                sort_x(g + 2)
+            quantise_u(g)
 
         gain_cols = keep.tile([P, D_GROUPS, PACK], F32, name="gain_cols")
         shift_cols = keep.tile([P, D_GROUPS, PACK], F32, name="shift_cols")
 
         for g in range(S_PASSES - LAG, S_PASSES - 1):
             moment_matmuls(g, 0)
-        moment_matmuls(0, 1)
-        interleave_cov_scalar(1, 1, SCALAR_UNITS)
-        interleave_cov_vector(1, 1, SCALAR_UNITS)
-        quantise_u(S_PASSES - 1)
         moment_matmuls(S_PASSES - 1, 0)
+        interleave_cov_scalar(1, 1, UNITS_A)
+        quantise_cov(0, 1)
+        moment_matmuls(0, 1)
+        interleave_cov_scalar(2, 1, SU_FIRST)
+        if SU_FIRST < UNITS:
+            interleave_cov_vector(2, 1, SU_FIRST)
+        quantise_cov(1, 1)
+        moment_matmuls(1, 1)
         nc.vector.tensor_copy(out=gain_cols[:], in_=gain_raw[:])
         nc.vector.tensor_tensor(out=shift_cols[:], in0=prior_raw[:], in1=gain_raw[:], op=ALU.mult)
         whole = slice(0, R)
-        for g in range(1, S_PASSES):
+        for g in range(2, S_PASSES):
+            if g == FIN:
+                for s in range(PACK):
+                    finish_slot(0, s, whole, True)
             if g + 1 < S_PASSES:
                 interleave_cov_scalar(g + 1, 1, SCALAR_UNITS)
                 interleave_cov_vector(g + 1, 1, SCALAR_UNITS)
-            if g == PL0 or (PL0 == 16 and g == 6):
+            if g == PL0:
                 interleave_y(0, whole)
             quantise_cov(g, 1)
-            if g == PL0 or (PL0 == 16 and g == 7):
+            if g == PL0:
                 store_planes(0, whole)
             moment_matmuls(g, 1)
-            if 1 <= g < 3:
-                finish_slot(0, 2 * g - 2, whole, True)
-                finish_slot(0, 2 * g - 1, whole, True)
-            if g == 3:
+            if g == TURN:
                 for rt in range(R_TILES):
                     turn_y(0, rt)
-            if g >= 4:
-                store_y(0, g - 4, True)
+            if g == TURN + 1 or g == TURN + 2:
+                store_y(0, 2 * (g - TURN - 1), True)
+                store_y(0, 2 * (g - TURN - 1) + 1, True)
         if PL0 == 8:
             interleave_y(0, whole)
             store_planes(0, whole)

@@ -25,15 +25,19 @@ D_GROUPS = D // K_PASS
 R_TILES = R // P
 EARLY_PASSES = 3
 UNITS = K_PASS // 8
-SCALAR_UNITS = 22
+WIDE = PACK * K_PASS
+SCALAR_UNITS = 20
 HEAD = 0
 FIRST_ON_SCALAR = 2
 COEF_Q = 0
-LAG = 2
-UNITS_A = 34
+LAG = 4
+UNITS_A = 36
 LB = 3
+G_UNITS = 28
+HLATE = 1
+TAILV = 0
 SU_FIRST = 32
-FIN = 3
+FIN = 4
 SPLIT = 0
 TURN = 4
 CB = 2
@@ -72,10 +76,10 @@ def tile_ipw_outcome_moments_k5_kernel(
         warm = keep.tile([P, 1], F32, name="warm")
         warm_out = keep.tile([P, 1], F32, name="warm_out")
 
-        nc.vector.memset(warm[:], 0.0)
         nc.vector.memset(h_rows[:], 0.0)
         nc.vector.memset(xs_early[:].bitcast(I32), 0)
         nc.vector.memset(coef_plane[:].bitcast(I32), 0)
+        nc.vector.memset(warm[:], 0.0)
         nc.vector.memset(xs_late[:].bitcast(I32), 0)
         nc.scalar.activation(out=warm_out[:], in_=warm[:], func=ACT.Exp)
         make_identity(nc, ident[:])
@@ -107,7 +111,7 @@ def tile_ipw_outcome_moments_k5_kernel(
         load_x(0)
         nc.sync.dma_start(out=h_rows[0:S_PASSES, :], in_=h.rearrange("(g s) -> g s", g=S_PASSES))
         load_scale_rows(xs_early, x_scales[:, :, :early], nc.sync)
-        load_scale_rows(coef_plane, coef_scales, nc.gpsimd if COEF_Q else nc.sync)
+        load_scale_rows(coef_plane, coef_scales, nc.sync)
         if HEAD == 0:
             load_cov(0, 0)
         load_x(1)
@@ -125,7 +129,8 @@ def tile_ipw_outcome_moments_k5_kernel(
             load_cov(g, 1)
 
         x_codes, x_plane, logits, expo = {}, {}, {}, {}
-        u_rows, u_words, u_codes, u_plane = {}, {}, {}, {}
+        pair, u_codes, u_plane = {}, {}, {}
+        pieces = [(g, dg) for dg in range(D_GROUPS) for g in range(S_PASSES)]
         c_words, c_codes, c_plane, moment = {}, {}, {}, {}
 
         def sort_x(g):
@@ -166,33 +171,36 @@ def tile_ipw_outcome_moments_k5_kernel(
                 func=ACT.Exp, scale=-1.0,
             )
 
+        def new_pair(g):
+            pair[g] = ring.tile([P, 2 * WIDE], BF16, name="pair", bufs=2, align_bytes=64)
+            c_words[pieces[g + 1]] = pair[g][:, WIDE:]
+
         def weight_u(g):
-            u_words[g] = ring.tile([P, R * PACK], BF16, name="u_words", bufs=2, align_bytes=64)
             nc.vector.scalar_tensor_tensor(
-                out=u_words[g][:].rearrange("p (r t) -> p r t", t=PACK), in0=expo[g][:], scalar=1.0,
+                out=pair[g][:, :WIDE].rearrange("p (r t) -> p r t", t=PACK), in0=expo[g][:], scalar=1.0,
                 in1=h_turned[:, g : g + 1, :].to_broadcast([P, R, PACK]), op0=ALU.add, op1=ALU.mult,
             )
 
-        def quantise_u(g):
-            u_codes[g] = keep.tile([P, R], U32, name="u_codes%d" % g, align_bytes=64)
-            u_plane[g] = keep.tile([P, R], U8, name="u_plane%d" % g, align_bytes=64)
-            nc.vector.quantize_mx(out=u_codes[g][:].bitcast(FP8X4), scales=u_plane[g][:], in_=u_words[g][:])
-
-        def new_cov_words(g, dg, name, bufs):
-            c_words[g, dg] = ring.tile([P, K_PASS * PACK], BF16, name=name, bufs=bufs, align_bytes=64)
+        def quantise_pair(g):
+            codes = keep.tile([P, 2 * R], U32, name="pair_codes%d" % g, align_bytes=64)
+            plane = keep.tile([P, 2 * R], U8, name="pair_plane%d" % g, align_bytes=64)
+            nc.vector.quantize_mx(out=codes[:].bitcast(FP8X4), scales=plane[:], in_=pair[g][:])
+            u_codes[g], u_plane[g] = codes[:, :R], plane[:, :R]
+            c_codes[pieces[g + 1]], c_plane[pieces[g + 1]] = codes[:, R:], plane[:, R:]
 
         def interleave_cov_gpsimd(g, dg, units):
-            dst = c_words[g, dg][:].rearrange("p (s m t) -> p s m t", s=PACK, t=PACK)
+            dst = c_words[g, dg].rearrange("p (s m t) -> p s m t", s=PACK, t=PACK)
             src = cov_raw[g, dg].rearrange("p t (m s) -> p s m t", s=PACK)
             nc.gpsimd.tensor_scalar(
-                out=dst[:, :, 2 * units :, :], in0=src[:, :, 2 * units :, :], scalar1=1.0, scalar2=0.0,
+                out=dst[:, :, 2 * (UNITS - units) :, :], in0=src[:, :, 2 * (UNITS - units) :, :], scalar1=1.0, scalar2=0.0,
                 op0=ALU.mult, op1=ALU.add,
             )
 
         def cov_views(g, dg):
             if (g, dg) not in c_words:
-                new_cov_words(g, dg, "c_words", 3)
-            dst = c_words[g, dg][:].rearrange("p (s n m t) -> p n t m s", s=PACK, m=2, t=PACK)
+                words = ring.tile([P, WIDE], BF16, name="c_words", bufs=3, align_bytes=64)
+                c_words[g, dg] = words[:]
+            dst = c_words[g, dg].rearrange("p (s n m t) -> p n t m s", s=PACK, m=2, t=PACK)
             src = cov_raw[g, dg].rearrange("p t (n m s) -> p n t m s", m=2, s=PACK)
             return dst, src
 
@@ -200,16 +208,15 @@ def tile_ipw_outcome_moments_k5_kernel(
             dst, src = cov_views(g, dg)
             nc.scalar.copy(out=dst[:, :units], in_=src[:, :units])
 
-        def interleave_cov_vector(g, dg, units):
+        def interleave_cov_vector(g, dg, units, stop=UNITS):
             dst, src = cov_views(g, dg)
-            nc.vector.tensor_copy(out=dst[:, units:], in_=src[:, units:])
+            nc.vector.tensor_copy(out=dst[:, units:stop], in_=src[:, units:stop])
 
         def quantise_cov(g, dg):
-            c_codes[g, dg] = ring.tile([P, K_PASS], U32, name="c_codes%d" % dg, bufs=5, align_bytes=64)
-            c_plane[g, dg] = ring.tile([P, K_PASS], U8, name="c_plane%d" % dg, bufs=5, align_bytes=64)
-            nc.vector.quantize_mx(
-                out=c_codes[g, dg][:].bitcast(FP8X4), scales=c_plane[g, dg][:], in_=c_words[g, dg][:]
-            )
+            codes = ring.tile([P, K_PASS], U32, name="c_codes", bufs=4, align_bytes=64)
+            plane = ring.tile([P, K_PASS], U8, name="c_plane", bufs=4, align_bytes=64)
+            nc.vector.quantize_mx(out=codes[:].bitcast(FP8X4), scales=plane[:], in_=c_words[g, dg])
+            c_codes[g, dg], c_plane[g, dg] = codes[:], plane[:]
 
         def moment_matmuls(g, dg):
             for s in range(PACK):
@@ -219,8 +226,8 @@ def tile_ipw_outcome_moments_k5_kernel(
                     out=moment[dg, s][:],
                     lhsT=c_codes[g, dg][:, P * s : P * (s + 1)].bitcast(FP8X4),
                     lhsT_scale=c_plane[g, dg][:, P * s : P * (s + 1)],
-                    rhs=u_codes[g][:].bitcast(FP8X4),
-                    rhs_scale=u_plane[g][:],
+                    rhs=u_codes[g].bitcast(FP8X4),
+                    rhs_scale=u_plane[g],
                     start=(g == 0),
                     stop=(g == S_PASSES - 1),
                 )
@@ -247,7 +254,7 @@ def tile_ipw_outcome_moments_k5_kernel(
                 nc.tensor.transpose(y_turned[dg, rt][:, s, :], y_rows[dg][:, s, P * rt : P * (rt + 1)], ident[:])
 
         def store_y(dg, rt, on_scalar):
-            y_out = ring.tile([P, K_PASS], F32, name="y_out", bufs=6)
+            y_out = ring.tile([P, K_PASS], F32, name="y_out", bufs=5)
             dst = y_out[:].rearrange("p (m s) -> p m s", s=PACK)
             src = y_turned[dg, rt][:].rearrange("p s m -> p m s")
             if on_scalar:
@@ -263,18 +270,20 @@ def tile_ipw_outcome_moments_k5_kernel(
                 in_=y_rows[dg][:].rearrange("p s (c i) -> p c s i", i=4),
             )
 
+        y_plane = keep.tile([P, D_GROUPS, R], U8, name="y_plane", align_bytes=64)
+
         def store_planes(dg, cols):
             y_codes = keep.tile([P, R], U32, name="y_codes%d" % dg, align_bytes=64)
-            y_plane = keep.tile([P, R], U8, name="y_plane%d" % dg, align_bytes=64)
-            nc.vector.quantize_mx(out=y_codes[:].bitcast(FP8X4), scales=y_plane[:], in_=y_words[dg][:])
+            nc.vector.quantize_mx(out=y_codes[:].bitcast(FP8X4), scales=y_plane[:, dg, :], in_=y_words[dg][:])
             nc.sync.dma_start(
                 out=out_1[dg].rearrange("p m t -> p (m t)").bitcast(I32), in_=y_codes[:].bitcast(I32)
             )
-            for q in range(4):
-                nc.sync.dma_start(
-                    out=out_2[dg, 4 * q : 4 * q + 4, :].bitcast(I32),
-                    in_=y_plane[32 * q : 32 * q + 4, :].bitcast(I32),
-                )
+            if dg == D_GROUPS - 1:
+                for q in range(4):
+                    nc.sync.dma_start(
+                        out=out_2[:, 4 * q : 4 * q + 4, :].rearrange("g r n -> r g n").bitcast(I32),
+                        in_=y_plane[32 * q : 32 * q + 4, :, :].bitcast(I32),
+                    )
 
         h_sorted = keep.tile([P, PACK, P], F32, name="h_sorted")
         nc.scalar.copy(
@@ -287,12 +296,11 @@ def tile_ipw_outcome_moments_k5_kernel(
         sort_x(0)
         for rt in range(LB):
             logit_matmuls(0, rt)
-        new_cov_words(0, 0, "c_shared", CB)
         interleave_cov_vector(0, 0, 0)
         sort_x(1)
-        pieces = [(g, dg) for dg in range(D_GROUPS) for g in range(S_PASSES)]
-        new_cov_words(1, 0, "c_shared", CB)
+        new_pair(0)
         interleave_cov_vector(1, 0, 0)
+        quantise_cov(0, 0)
 
         for g in range(S_PASSES):
             for rt in range(R_TILES):
@@ -302,15 +310,16 @@ def tile_ipw_outcome_moments_k5_kernel(
                     logit_matmuls(ahead // R_TILES, ahead % R_TILES)
             if g >= LAG:
                 moment_matmuls(g - LAG, 0)
-            quantise_cov(g, 0)
-            new_cov_words(*pieces[g + 2], "c_shared", CB)
+            new_pair(g + 1)
             weight_u(g)
-            interleave_cov_gpsimd(*pieces[g + 2], UNITS_A)
+            interleave_cov_gpsimd(*pieces[g + 2], G_UNITS)
             if g >= 1:
                 interleave_cov_scalar(*pieces[g + 1], UNITS_A)
+            if UNITS_A + G_UNITS < UNITS:
+                interleave_cov_vector(*pieces[g + 2], UNITS_A, UNITS - G_UNITS)
             if g + 2 < S_PASSES:
                 sort_x(g + 2)
-            quantise_u(g)
+            quantise_pair(g)
 
         gain_cols = keep.tile([P, D_GROUPS, PACK], F32, name="gain_cols")
         shift_cols = keep.tile([P, D_GROUPS, PACK], F32, name="shift_cols")
@@ -319,7 +328,6 @@ def tile_ipw_outcome_moments_k5_kernel(
             moment_matmuls(g, 0)
         moment_matmuls(S_PASSES - 1, 0)
         interleave_cov_scalar(1, 1, UNITS_A)
-        quantise_cov(0, 1)
         moment_matmuls(0, 1)
         interleave_cov_scalar(2, 1, SU_FIRST)
         if SU_FIRST < UNITS:
@@ -362,8 +370,8 @@ def tile_ipw_outcome_moments_k5_kernel(
             interleave_y(1, whole)
             store_y(1, 1, True)
             store_y(1, 2, True)
-            store_planes(1, whole)
             store_y(1, 3, True)
+            store_planes(1, whole)
         if TAIL == 1:
             store_y(1, 0, True)
             store_y(1, 1, False)

from contextlib import ExitStack

import concourse.mybir as mybir
from concourse.masks import make_identity

S, K, R, D = 4096, 1024, 512, 1024
FLOPS = 2 * S * K * R + 2 * S * R * D

F32 = mybir.dt.float32
BF16 = mybir.dt.bfloat16
I32 = mybir.dt.int32
U32 = mybir.dt.uint32
U8 = mybir.dt.uint8
FP8X4 = mybir.dt.float8_e4m3fn_x4
FP4X4 = mybir.dt.float4_e2m1fn_x4
ACT = mybir.ActivationFunctionType
ALU = mybir.AluOpType

P = 128
PACK = 4
K_PASS = P * PACK
K_PASSES = K // K_PASS
S_PASSES = S // K_PASS
D_GROUPS = D // K_PASS
R_TILES = R // P
EARLY_PASSES = 3
UNITS = K_PASS // 8
WIDE = PACK * K_PASS
SCALAR_UNITS = 20
HEAD = 0
FIRST_ON_SCALAR = 2
COEF_Q = 0
LAG = 4
UNITS_A = 36
LB = 3
G_UNITS = 28
HLATE = 1
TAILV = 0
SU_FIRST = 32
FIN = 4
SPLIT = 0
TURN = 4
CB = 2
HEAD_UNITS = 24
XFIRST = 0
TAIL = 0
PL0 = 7
S_EVEN = 3
S_ODD = 4


def tile_ipw_outcome_moments_k5_kernel(
    tc, x_words, x_scales, coef_words, coef_scales, h, cov, prior, gain, out_0, out_1, out_2
):
    nc = tc.nc
    with ExitStack() as ctx:
        keep = ctx.enter_context(tc.tile_pool(name="keep", bufs=1))
        ring = ctx.enter_context(tc.tile_pool(name="ring", bufs=1))
        psum = ctx.enter_context(tc.psum_pool(name="psum", bufs=1))
        ctx.enter_context(tc.manual_schedule())

        def bank(b, shape):
            return psum.tile(shape, F32, name="bank%d" % b, tag="bank%d" % b)

        coef_codes = keep.tile([P, K_PASSES, 2 * R], U8, name="coef_codes", align_bytes=64)
        coef_plane = keep.tile([P, K_PASSES, R], U8, name="coef_plane", align_bytes=64)
        x_raw = [keep.tile([P, K_PASSES, 2 * K_PASS], U8, name="x_raw%d" % g) for g in range(S_PASSES)]
        early = EARLY_PASSES * K_PASS
        xs_early = keep.tile([P, K_PASSES, early], U8, name="xs_early")
        xs_late = keep.tile([P, K_PASSES, S - early], U8, name="xs_late")
        cov_raw = {}
        h_rows = keep.tile([P, K_PASS], BF16, name="h_rows")
        prior_raw = keep.tile([P, D_GROUPS, PACK], BF16, name="prior_raw")
        gain_raw = keep.tile([P, D_GROUPS, PACK], BF16, name="gain_raw")
        ident = keep.tile([P, P], F32, name="ident")
        warm = keep.tile([P, 1], F32, name="warm")
        warm_out = keep.tile([P, 1], F32, name="warm_out")

        nc.vector.memset(h_rows[:], 0.0)
        nc.vector.memset(xs_early[:].bitcast(I32), 0)
        nc.vector.memset(coef_plane[:].bitcast(I32), 0)
        nc.vector.memset(warm[:], 0.0)
        nc.vector.memset(xs_late[:].bitcast(I32), 0)
        nc.scalar.activation(out=warm_out[:], in_=warm[:], func=ACT.Exp)
        make_identity(nc, ident[:])

        def load_scale_rows(plane, rows, queue):
            for q in range(4):
                queue.dma_start(
                    out=plane[32 * q : 32 * q + 4, :, :].bitcast(I32),
                    in_=rows[:, 4 * q : 4 * q + 4, :].rearrange("k r n -> r k n").bitcast(I32),
                )

        def load_x(g):
            cols = slice(2 * K_PASS * g, 2 * K_PASS * (g + 1))
            nc.sync.dma_start(
                out=x_raw[g][:].bitcast(I32), in_=x_words[:, :, cols].rearrange("k p n -> p k n").bitcast(I32)
            )

        def load_cov_rows(dst, g, cols):
            rows = cov[K_PASS * g : K_PASS * (g + 1), cols].rearrange("(u t e) d -> e u t d", t=PACK, e=4)
            for e in range(4):
                nc.sync.dma_start(out=dst[e:P:4, :, :], in_=rows[e])

        def load_cov(g, dg):
            piece = keep.tile([P, PACK, K_PASS], BF16, name="cov_raw%d_%d" % (g, dg))
            load_cov_rows(piece, g, slice(K_PASS * dg, K_PASS * (dg + 1)))
            cov_raw[g, dg] = piece[:]

        nc.sync.dma_start(out=coef_codes[:].bitcast(I32), in_=coef_words.rearrange("k p n -> p k n").bitcast(I32))
        load_x(0)
        nc.sync.dma_start(out=h_rows[0:S_PASSES, :], in_=h.rearrange("(g s) -> g s", g=S_PASSES))
        load_scale_rows(xs_early, x_scales[:, :, :early], nc.sync)
        load_scale_rows(coef_plane, coef_scales, nc.sync)
        if HEAD == 0:
            load_cov(0, 0)
        load_x(1)
        for g in range(1, S_PASSES):
            if XFIRST and g + 1 < S_PASSES:
                load_x(g + 1)
            load_cov(g, 0)
            if g + 1 == EARLY_PASSES:
                load_scale_rows(xs_late, x_scales[:, :, early:], nc.sync)
            if not XFIRST and g + 1 < S_PASSES:
                load_x(g + 1)
        nc.sync.dma_start(out=prior_raw[:], in_=prior.rearrange("(g p t) -> p g t", p=P, t=PACK))
        nc.sync.dma_start(out=gain_raw[:], in_=gain.rearrange("(g p t) -> p g t", p=P, t=PACK))
        for g in range(S_PASSES):
            load_cov(g, 1)

        x_codes, x_plane, logits, expo = {}, {}, {}, {}
        pair, u_codes, u_plane = {}, {}, {}
        pieces = [(g, dg) for dg in range(D_GROUPS) for g in range(S_PASSES)]
        c_words, c_codes, c_plane, moment = {}, {}, {}, {}

        def sort_x(g):
            x_codes[g] = ring.tile([P, K_PASSES, 2 * K_PASS], U8, name="x_codes", bufs=3, align_bytes=64)
            x_plane[g] = ring.tile([P, K_PASSES, K_PASS], U8, name="x_plane", bufs=3, align_bytes=64)
            nc.vector.tensor_copy(
                out=x_codes[g][:].bitcast(I32).rearrange("p k (t u w) -> p k u t w", t=PACK, w=2),
                in_=x_raw[g][:].bitcast(I32).rearrange("p k (u t w) -> p k u t w", t=PACK, w=2),
            )
            if g < EARLY_PASSES:
                src = xs_early[:, :, K_PASS * g : K_PASS * (g + 1)]
            else:
                src = xs_late[:, :, K_PASS * g - early : K_PASS * (g + 1) - early]
            nc.vector.tensor_copy(
                out=x_plane[g][:].bitcast(I32).rearrange("p k (t u) -> p k u t", t=PACK),
                in_=src.bitcast(I32).rearrange("p k (u t) -> p k u t", t=PACK),
            )

        def logit_matmuls(g, rt):
            logits[g, rt] = bank(8 - LB + (R_TILES * g + rt) % LB, [P, PACK, P])
            for t in range(PACK):
                for k in range(K_PASSES):
                    nc.tensor.matmul_mx(
                        out=logits[g, rt][:, t, :],
                        lhsT=x_codes[g][:, k, 2 * P * t : 2 * P * (t + 1)].bitcast(FP4X4),
                        lhsT_scale=x_plane[g][:, k, P * t : P * (t + 1)],
                        rhs=coef_codes[:, k, 2 * P * rt : 2 * P * (rt + 1)].bitcast(FP4X4),
                        rhs_scale=coef_plane[:, k, P * rt : P * (rt + 1)],
                        start=(k == 0),
                        stop=(k == K_PASSES - 1),
                    )

        def exp_tile(g, rt):
            if rt == 0:
                expo[g] = ring.tile([P, R, PACK], F32, name="expo", bufs=2)
            nc.scalar.activation(
                out=expo[g][:, P * rt : P * (rt + 1), :], in_=logits[g, rt][:].rearrange("p t r -> p r t"),
                func=ACT.Exp, scale=-1.0,
            )

        def new_pair(g):
            pair[g] = ring.tile([P, 2 * WIDE], BF16, name="pair", bufs=2, align_bytes=64)
            c_words[pieces[g + 1]] = pair[g][:, WIDE:]

        def weight_u(g):
            nc.vector.scalar_tensor_tensor(
                out=pair[g][:, :WIDE].rearrange("p (r t) -> p r t", t=PACK), in0=expo[g][:], scalar=1.0,
                in1=h_turned[:, g : g + 1, :].to_broadcast([P, R, PACK]), op0=ALU.add, op1=ALU.mult,
            )

        def quantise_pair(g):
            codes = keep.tile([P, 2 * R], U32, name="pair_codes%d" % g, align_bytes=64)
            plane = keep.tile([P, 2 * R], U8, name="pair_plane%d" % g, align_bytes=64)
            nc.vector.quantize_mx(out=codes[:].bitcast(FP8X4), scales=plane[:], in_=pair[g][:])
            u_codes[g], u_plane[g] = codes[:, :R], plane[:, :R]
            c_codes[pieces[g + 1]], c_plane[pieces[g + 1]] = codes[:, R:], plane[:, R:]

        def interleave_cov_gpsimd(g, dg, units):
            dst = c_words[g, dg].rearrange("p (s m t) -> p s m t", s=PACK, t=PACK)
            src = cov_raw[g, dg].rearrange("p t (m s) -> p s m t", s=PACK)
            nc.gpsimd.tensor_scalar(
                out=dst[:, :, 2 * (UNITS - units) :, :], in0=src[:, :, 2 * (UNITS - units) :, :], scalar1=1.0, scalar2=0.0,
                op0=ALU.mult, op1=ALU.add,
            )

        def cov_views(g, dg):
            if (g, dg) not in c_words:
                words = ring.tile([P, WIDE], BF16, name="c_words", bufs=3, align_bytes=64)
                c_words[g, dg] = words[:]
            dst = c_words[g, dg].rearrange("p (s n m t) -> p n t m s", s=PACK, m=2, t=PACK)
            src = cov_raw[g, dg].rearrange("p t (n m s) -> p n t m s", m=2, s=PACK)
            return dst, src

        def interleave_cov_scalar(g, dg, units):
            dst, src = cov_views(g, dg)
            nc.scalar.copy(out=dst[:, :units], in_=src[:, :units])

        def interleave_cov_vector(g, dg, units, stop=UNITS):
            dst, src = cov_views(g, dg)
            nc.vector.tensor_copy(out=dst[:, units:stop], in_=src[:, units:stop])

        def quantise_cov(g, dg):
            codes = ring.tile([P, K_PASS], U32, name="c_codes", bufs=4, align_bytes=64)
            plane = ring.tile([P, K_PASS], U8, name="c_plane", bufs=4, align_bytes=64)
            nc.vector.quantize_mx(out=codes[:].bitcast(FP8X4), scales=plane[:], in_=c_words[g, dg])
            c_codes[g, dg], c_plane[g, dg] = codes[:], plane[:]

        def moment_matmuls(g, dg):
            for s in range(PACK):
                if g == 0:
                    moment[dg, s] = bank(4 * dg + s, [P, R])
                nc.tensor.matmul_mx(
                    out=moment[dg, s][:],
                    lhsT=c_codes[g, dg][:, P * s : P * (s + 1)].bitcast(FP8X4),
                    lhsT_scale=c_plane[g, dg][:, P * s : P * (s + 1)],
                    rhs=u_codes[g].bitcast(FP8X4),
                    rhs_scale=u_plane[g],
                    start=(g == 0),
                    stop=(g == S_PASSES - 1),
                )

        y_rows, y_turned, y_words = {}, {}, {}

        def finish_slot(dg, s, cols, on_scalar):
            if dg not in y_rows:
                y_rows[dg] = keep.tile([P, PACK, R], F32, name="y_rows%d" % dg)
            if on_scalar:
                nc.scalar.activation(
                    out=y_rows[dg][:, s, cols], in_=moment[dg, s][:, cols], func=ACT.Identity,
                    scale=gain_cols[:, dg, s : s + 1], bias=shift_cols[:, dg, s : s + 1],
                )
            else:
                nc.vector.tensor_scalar(
                    out=y_rows[dg][:, s, cols], in0=moment[dg, s][:, cols], scalar1=gain_cols[:, dg, s : s + 1],
                    scalar2=shift_cols[:, dg, s : s + 1], op0=ALU.mult, op1=ALU.add,
                )

        def turn_y(dg, rt):
            y_turned[dg, rt] = bank(rt, [P, PACK, P])
            for s in range(PACK):
                nc.tensor.transpose(y_turned[dg, rt][:, s, :], y_rows[dg][:, s, P * rt : P * (rt + 1)], ident[:])

        def store_y(dg, rt, on_scalar):
            y_out = ring.tile([P, K_PASS], F32, name="y_out", bufs=5)
            dst = y_out[:].rearrange("p (m s) -> p m s", s=PACK)
            src = y_turned[dg, rt][:].rearrange("p s m -> p m s")
            if on_scalar:
                nc.scalar.copy(out=dst, in_=src)
            else:
                nc.vector.tensor_copy(out=dst, in_=src)
            nc.sync.dma_start(out=out_0[P * rt : P * (rt + 1), K_PASS * dg : K_PASS * (dg + 1)], in_=y_out[:])

        def interleave_y(dg, cols):
            y_words[dg] = ring.tile([P, R * PACK], BF16, name="y_words", bufs=2, align_bytes=64)
            nc.vector.tensor_copy(
                out=y_words[dg][:].rearrange("p (c i s) -> p c s i", i=4, s=PACK),
                in_=y_rows[dg][:].rearrange("p s (c i) -> p c s i", i=4),
            )

        y_plane = keep.tile([P, D_GROUPS, R], U8, name="y_plane", align_bytes=64)

        def store_planes(dg, cols):
            y_codes = keep.tile([P, R], U32, name="y_codes%d" % dg, align_bytes=64)
            nc.vector.quantize_mx(out=y_codes[:].bitcast(FP8X4), scales=y_plane[:, dg, :], in_=y_words[dg][:])
            nc.sync.dma_start(
                out=out_1[dg].rearrange("p m t -> p (m t)").bitcast(I32), in_=y_codes[:].bitcast(I32)
            )
            if dg == D_GROUPS - 1:
                for q in range(4):
                    nc.sync.dma_start(
                        out=out_2[:, 4 * q : 4 * q + 4, :].rearrange("g r n -> r g n").bitcast(I32),
                        in_=y_plane[32 * q : 32 * q + 4, :, :].bitcast(I32),
                    )

        h_sorted = keep.tile([P, PACK, P], F32, name="h_sorted")
        nc.scalar.copy(
            out=h_sorted[:].rearrange("p t (u e) -> p t u e", e=4),
            in_=h_rows[:].rearrange("p (u t e) -> p t u e", t=PACK, e=4),
        )
        h_turned = bank(4, [P, P, PACK])
        for t in range(PACK):
            nc.tensor.transpose(h_turned[:, :, t], h_sorted[:, t, :], ident[:])
        sort_x(0)
        for rt in range(LB):
            logit_matmuls(0, rt)
        interleave_cov_vector(0, 0, 0)
        sort_x(1)
        new_pair(0)
        interleave_cov_vector(1, 0, 0)
        quantise_cov(0, 0)

        for g in range(S_PASSES):
            for rt in range(R_TILES):
                exp_tile(g, rt)
                ahead = R_TILES * g + rt + LB
                if ahead < R_TILES * S_PASSES:
                    logit_matmuls(ahead // R_TILES, ahead % R_TILES)
            if g >= LAG:
                moment_matmuls(g - LAG, 0)
            new_pair(g + 1)
            weight_u(g)
            interleave_cov_gpsimd(*pieces[g + 2], G_UNITS)
            if g >= 1:
                interleave_cov_scalar(*pieces[g + 1], UNITS_A)
            if UNITS_A + G_UNITS < UNITS:
                interleave_cov_vector(*pieces[g + 2], UNITS_A, UNITS - G_UNITS)
            if g + 2 < S_PASSES:
                sort_x(g + 2)
            quantise_pair(g)

        gain_cols = keep.tile([P, D_GROUPS, PACK], F32, name="gain_cols")
        shift_cols = keep.tile([P, D_GROUPS, PACK], F32, name="shift_cols")

        for g in range(S_PASSES - LAG, S_PASSES - 1):
            moment_matmuls(g, 0)
        moment_matmuls(S_PASSES - 1, 0)
        interleave_cov_scalar(1, 1, UNITS_A)
        moment_matmuls(0, 1)
        interleave_cov_scalar(2, 1, SU_FIRST)
        if SU_FIRST < UNITS:
            interleave_cov_vector(2, 1, SU_FIRST)
        quantise_cov(1, 1)
        moment_matmuls(1, 1)
        nc.vector.tensor_copy(out=gain_cols[:], in_=gain_raw[:])
        nc.vector.tensor_tensor(out=shift_cols[:], in0=prior_raw[:], in1=gain_raw[:], op=ALU.mult)
        whole = slice(0, R)
        for g in range(2, S_PASSES):
            if g == FIN:
                for s in range(PACK):
                    finish_slot(0, s, whole, True)
            if g + 1 < S_PASSES:
                interleave_cov_scalar(g + 1, 1, SCALAR_UNITS)
                interleave_cov_vector(g + 1, 1, SCALAR_UNITS)
            if g == PL0:
                interleave_y(0, whole)
            quantise_cov(g, 1)
            if g == PL0:
                store_planes(0, whole)
            moment_matmuls(g, 1)
            if g == TURN:
                for rt in range(R_TILES):
                    turn_y(0, rt)
            if g == TURN + 1 or g == TURN + 2:
                store_y(0, 2 * (g - TURN - 1), True)
                store_y(0, 2 * (g - TURN - 1) + 1, True)
        if PL0 == 8:
            interleave_y(0, whole)
            store_planes(0, whole)
        halves = [slice(0, R // 2), slice(R // 2, R)]
        for half in range(2):
            for s in range(PACK):
                finish_slot(1, s, halves[half], s % 2 == 0)
            for rt in range(2 * half, 2 * half + 2):
                turn_y(1, rt)
        if TAIL == 0:
            store_y(1, 0, True)
            interleave_y(1, whole)
            store_y(1, 1, True)
            store_y(1, 2, True)
            store_y(1, 3, True)
            store_planes(1, whole)
        if TAIL == 1:
            store_y(1, 0, True)
            store_y(1, 1, False)
            interleave_y(1, whole)
            store_y(1, 2, True)
            store_y(1, 3, True)
            store_planes(1, whole)
